import numpy as np
import ml_dtypes


def mxq(x, axis, fmt="e4m3"):
    dtype, down = {"e4m3": (ml_dtypes.float8_e4m3fn, 7), "e5m2": (ml_dtypes.float8_e5m2, 14)}[fmt]
    v = np.moveaxis(np.asarray(x, np.float32).astype(ml_dtypes.bfloat16).astype(np.float64), axis, -1)
    blocks = v.reshape(v.shape[:-1] + (-1, 32))
    amax = np.abs(blocks).max(-1, keepdims=True)
    byte = np.maximum(np.where(amax > 0, np.frexp(amax)[1] - 1 + 127, 0) - down, 1)
    scale = np.exp2(byte - 127.0)
    codes = (blocks / scale).astype(np.float32).astype(dtype).astype(np.float64)
    return np.moveaxis((codes * scale).reshape(v.shape), -1, axis)


WIDE = False


def mx_kscale(k):
    if not WIDE:
        return np.ones(k)
    levels = np.array([10, -10, 5, -5, 0])
    if k % 512:
        return np.exp2(np.random.permutation(np.resize(levels, k // 32))).repeat(32)
    a = np.empty((k // 512, 16))
    for p in range(k // 512):
        a[p, :8] = np.random.permutation(np.resize(levels, 8))
        for g in range(8):
            far = levels[np.abs(levels - a[p, g]) >= 10]
            a[p, g + 8] = far[np.random.randint(len(far))]
    return np.exp2(a.ravel()).repeat(32)


def f64(x):
    return np.asarray(x).astype(np.float64)


def striped(idx):
    return np.tile(idx.reshape(-1, 16).T, (8, 1)).astype(np.uint16)


def unstriped(offs):
    return offs[:16].T.reshape(-1).astype(np.int64)


E2M1 = np.array([0.0, 0.5, 1.0, 1.5, 2.0, 3.0, 4.0, 6.0, -0.0, -0.5, -1.0, -1.5, -2.0, -3.0, -4.0, -6.0])


def pack_weight(w, fmt):
    k, n = w.shape
    w = f64(np.asarray(w, np.float32).astype(ml_dtypes.bfloat16)).reshape(k // 32, 32, n)
    amax = np.abs(w).max(1)
    if fmt == "e4m3":
        byte = np.frexp(amax)[1] - 1 + 127 - 7
    else:
        mant, ex = np.frexp(amax / 6.0)
        byte = np.where(mant > 0.5, ex, ex - 1) + 127
    byte = np.clip(np.where(amax > 0, byte, 1), 1, 254)
    scaled = (w * np.exp2(127.0 - byte)[:, None, :]).reshape(k, n).astype(np.float32)
    by_word = np.ascontiguousarray(scaled.reshape(k // 512, 128, 4, n).transpose(0, 1, 3, 2))
    if fmt == "e4m3":
        words = by_word.astype(ml_dtypes.float8_e4m3fn).view(np.uint8)
    else:
        c = by_word.astype(ml_dtypes.float4_e2m1fn).view(np.uint8) & 0xF
        words = (c[..., 0::2] | (c[..., 1::2] << 4)).reshape(k // 512, 128, 2 * n)
    return np.ascontiguousarray(words), np.ascontiguousarray(byte.astype(np.uint8).reshape(k // 512, 16, n))


def unpack_weight(words, scales, fmt):
    g, _, n = scales.shape
    words = np.ascontiguousarray(words).reshape(g, 128, n, -1)
    if fmt == "e4m3":
        vals = words.view(ml_dtypes.float8_e4m3fn).astype(np.float64)
    else:
        nib = np.empty((g, 128, n, 4), np.uint8)
        nib[..., 0::2] = words & 0xF
        nib[..., 1::2] = words >> 4
        vals = E2M1[nib]
    vals = vals * np.repeat(np.exp2(scales.astype(np.float64) - 127.0), 8, axis=1)[..., None]
    return vals.transpose(0, 1, 3, 2).reshape(g * 512, n)


K, T, E, C, N = 256, 1024, 4, 128, 512


def by_expert(wq, xq):
    return np.concatenate([wq[e].T @ xq[:, e * C:(e + 1) * C] for e in range(E)], axis=1)


def setup_inputs():
    n = np.random.standard_normal
    v = mx_kscale(N)
    slot_token = np.random.permutation(T)[:E * C]
    w_slot = np.random.uniform(0.2, 1.0, E * C)
    dq = pack_weight(n((N, T)) * v[:, None], "e4m3")
    dk = pack_weight(n((N, T)) * v[:, None], "e4m3")
    dv = pack_weight(n((N, T)) * v[:, None], "e4m3")
    wq = [pack_weight(m, "e2m1") for m in n((E, N, K)) / np.sqrt(N) / v[None, :, None]]
    wk = [pack_weight(m, "e2m1") for m in n((E, N, K)) / np.sqrt(N) / v[None, :, None]]
    return {
        "dq_words": dq[0],
        "dq_scales": dq[1],
        "dk_words": dk[0],
        "dk_scales": dk[1],
        "dv_words": dv[0],
        "dv_scales": dv[1],
        "wq_words": np.stack([m[0] for m in wq]),
        "wq_scales": np.stack([m[1] for m in wq]),
        "wk_words": np.stack([m[0] for m in wk]),
        "wk_scales": np.stack([m[1] for m in wk]),
        "wv": (n((E, N, K)) / np.sqrt(N) / v[None, :, None]).astype(np.float32),
        "gate": (np.tile(w_slot, (128, 1))).astype(np.float32),
        "offs": striped(slot_token),
    }


def reference(dq_words, dq_scales, dk_words, dk_scales, dv_words, dv_scales, wq_words, wq_scales, wk_words, wk_scales, wv, gate, offs):
    wq = np.stack([unpack_weight(wq_words[e], wq_scales[e], "e2m1") for e in range(E)])
    wk = np.stack([unpack_weight(wk_words[e], wk_scales[e], "e2m1") for e in range(E)])
    wvq = mxq(f64(wv), 1, "e4m3")
    idx = unstriped(offs)
    gq, gk, gv = [unpack_weight(w, s, "e4m3")[:, idx] for w, s in ((dq_words, dq_scales), (dk_words, dk_scales), (dv_words, dv_scales))]
    dx = f64(gate[:1]) * (by_expert(wq, gq) + by_expert(wk, gk) + by_expert(wvq, gv))
    out = np.zeros((K, T))
    out[:, idx] = dx
    return out

@@ -1,0 +1,182 @@
+from contextlib import ExitStack
+
+import concourse.mybir as mybir
+
+K, T, E, C, N = 256, 1024, 4, 128, 512
+S = E * C
+FLOPS = 2 * 3 * N * K * S
+
+F32 = mybir.dt.float32
+BF16 = mybir.dt.bfloat16
+I32 = mybir.dt.int32
+U32 = mybir.dt.uint32
+U16 = mybir.dt.uint16
+U8 = mybir.dt.uint8
+FP8X4 = mybir.dt.float8_e4m3fn_x4
+FP4X4 = mybir.dt.float4_e2m1fn_x4
+MULT = mybir.AluOpType.mult
+
+P = 128
+PACK = 4
+HALVES = K // P
+W_ROWS = 4
+WARM = 64
+
+
+def tile_moe_qkb_kernel(
+    tc, dq_words, dq_scales, dk_words, dk_scales, dv_words, dv_scales,
+    wq_words, wq_scales, wk_words, wk_scales, wv, gate, offs, out,
+):
+    nc = tc.nc
+    with ExitStack() as ctx:
+        keep = ctx.enter_context(tc.tile_pool(name="keep", bufs=1))
+        psum = ctx.enter_context(tc.psum_pool(name="psum", bufs=1))
+
+        offsets = keep.tile([P, S // 16], U16, name="offsets")
+        nc.sync.dma_start(offsets[:], offs)
+
+        names = ("q", "k", "v")
+        g_words = dict(zip(names, (dq_words, dk_words, dv_words)))
+        g_scales = dict(zip(names, (dq_scales, dk_scales, dv_scales)))
+        tok_words = {n: keep.tile([P, T], I32, name="tok_words_" + n, align_bytes=64) for n in names}
+        tok_scales = {n: keep.tile([P, T], U8, name="tok_scales_" + n, align_bytes=64) for n in names}
+        slot_words = {n: keep.tile([P, S], U32, name="slot_words_" + n, align_bytes=64) for n in names}
+        slot_scales = {n: keep.tile([P, S], U8, name="slot_scales_" + n, align_bytes=64) for n in names}
+        w_words = {n: keep.tile([P, E, 2 * K], U8, name="w_words_" + n, align_bytes=64) for n in "qk"}
+        w_scales_both = keep.tile([P, 2, E, K], U8, name="w_scales_both", align_bytes=64)
+        wv_raw = [keep.tile([P, PACK, K], F32, name="wv_raw_%d" % e) for e in range(E)]
+        wv_bf = [keep.tile([P, K, PACK], BF16, name="wv_bf_%d" % e, align_bytes=64) for e in range(E)]
+        wv_codes = [keep.tile([P, K], U32, name="wv_codes_%d" % e, align_bytes=64) for e in range(E)]
+        wv_scales = [keep.tile([P, K], U8, name="wv_scales_%d" % e, align_bytes=64) for e in range(E)]
+        gate_sb = keep.tile([P, S], F32, name="gate_sb")
+        sums = [keep.tile([P, S], F32, name="sums_%d" % h) for h in range(HALVES)]
+        result = [keep.tile([P, T], F32, name="result_%d" % h) for h in range(HALVES)]
+        acc = [[psum.tile([P, C], F32, name="acc_%d_%d" % (e, h)) for h in range(HALVES)] for e in range(E)]
+
+        def load_words(n):
+            nc.sync.dma_start(tok_words[n][:], g_words[n][0].rearrange("p t d -> p (t d)").bitcast(I32))
+
+        def load_scales(n, queue, which):
+            rows = g_scales[n][0].rearrange("(q r) t -> r q t", r=4)
+            for r in which:
+                queue.dma_start(tok_scales[n][r:P:32, :].bitcast(I32), rows[r].bitcast(I32))
+
+        def load_wv(e):
+            nc.sync.dma_start(wv_raw[e][:], wv[e].rearrange("(p j) c -> p j c", j=PACK))
+
+        def load_w_words(n, src):
+            nc.sync.dma_start(w_words[n][:].bitcast(I32), src.rearrange("e s p b -> p (e s) b").bitcast(I32))
+
+        def load_w_scales(n, src):
+            rows = src.rearrange("e s (q r) c -> r q (e s) c", r=4)
+            for r in range(W_ROWS):
+                nc.gpsimd.dma_start(w_scales_both[r:P:32, "qk".index(n), :, :].bitcast(I32), rows[r].bitcast(I32))
+
+        def gather_words(n, a, b):
+            window = tok_words[n][:].bitcast(U32).indirect(offsets[:, a // 16 : b // 16])
+            nc.vector.tensor_copy(slot_words[n][:, a:b], window)
+
+        def gather_scales(n, a, b):
+            window = tok_scales[n][:].indirect(offsets[:, a // 16 : b // 16])
+            nc.vector.tensor_copy(slot_scales[n][:, a:b], window)
+
+        def interleave(e):
+            nc.scalar.copy(
+                wv_bf[e][:].rearrange("p (c i) j -> p c j i", i=4),
+                wv_raw[e][:].rearrange("p j (c i) -> p c j i", i=4),
+            )
+
+        def quantise(e):
+            nc.vector.quantize_mx(
+                out=wv_codes[e][:].bitcast(FP8X4),
+                scales=wv_scales[e][:],
+                in_=wv_bf[e][:].rearrange("p c j -> p (c j)"),
+            )
+
+        def product(n, e, h):
+            slots = slice(e * C, (e + 1) * C)
+            cols = slice(h * P, (h + 1) * P)
+            if n == "v":
+                lhsT, lhsT_scale = wv_codes[e][:, cols].bitcast(FP8X4), wv_scales[e][:, cols]
+            else:
+                lhsT = w_words[n][:, e, 2 * h * P : 2 * (h + 1) * P].bitcast(FP4X4)
+                lhsT_scale = w_scales_both[:, "qk".index(n), e, cols]
+            nc.tensor.matmul_mx(
+                out=acc[e][h][:], lhsT=lhsT, lhsT_scale=lhsT_scale,
+                rhs=slot_words[n][:, slots].bitcast(FP8X4), rhs_scale=slot_scales[n][:, slots],
+                start=(n == "q"), stop=(n == "v"),
+            )
+
+        def scatter(h, a, b):
+            window = result[h][:].indirect(offsets[:, a // 16 : b // 16])
+            nc.vector.tensor_tensor(window, sums[h][:, a:b], gate_sb[:, a:b], MULT)
+
+        def evacuate(e, h):
+            nc.scalar.copy(sums[h][:, e * C : (e + 1) * C], acc[e][h][:])
+
+        def finish(e):
+            for h in range(HALVES):
+                product("v", e, h)
+            for h in range(HALVES):
+                evacuate(e, h)
+
+        nc.vector.memset(tok_scales["q"][:].bitcast(I32), 0)
+        nc.vector.memset(result[0][:, :WARM], 0.0)
+        nc.vector.memset(w_scales_both[:].rearrange("p n e c -> p (n e c)").bitcast(I32), 0)
+        nc.vector.memset(tok_scales["k"][:].bitcast(I32), 0)
+        nc.vector.memset(tok_scales["v"][:].bitcast(I32), 0)
+        nc.vector.memset(result[0][:, WARM:], 0.0)
+        nc.vector.memset(result[1][:, WARM:], 0.0)
+
+        load_scales("q", nc.scalar, range(4))
+        nc.scalar.copy(result[1][:, :WARM], result[0][:, :WARM])
+        load_w_scales("q", wq_scales)
+        load_w_scales("k", wk_scales)
+
+        load_words("q")
+        load_words("k")
+        load_wv(0)
+        load_scales("k", nc.sync, (0, 1))
+        load_words("v")
+        load_scales("k", nc.sync, (2, 3))
+        load_wv(1)
+        load_scales("v", nc.sync, range(4))
+        load_w_words("q", wq_words)
+        load_w_words("k", wk_words)
+        load_wv(2)
+        nc.sync.dma_start(gate_sb[:], gate)
+        load_wv(3)
+
+        gather_words("q", 0, S)
+        gather_scales("q", 0, S)
+        gather_words("k", 0, S)
+        interleave(0)
+        quantise(0)
+        gather_words("v", 0, S)
+        gather_scales("k", 0, S)
+        interleave(1)
+        quantise(1)
+        gather_scales("v", 0, C)
+        gather_scales("v", C, S)
+
+        for n in "qk":
+            for e in range(E):
+                for h in range(HALVES):
+                    product(n, e, h)
+        finish(0)
+        finish(1)
+        scatter(0, 0, C)
+        scatter(0, C, 2 * C)
+        interleave(2)
+        quantise(2)
+        interleave(3)
+        quantise(3)
+        finish(2)
+        finish(3)
+        scatter(1, 0, C)
+        scatter(1, C, 2 * C)
+        scatter(0, 2 * C, 3 * C)
+        scatter(0, 3 * C, S)
+        nc.sync.dma_start(out[0:P, :], result[0][:])
+        scatter(1, 2 * C, S)
+        nc.sync.dma_start(out[P : 2 * P, :], result[1][:])

@@ -19,7 +19,6 @@ MULT = mybir.AluOpType.mult
 P = 128
 PACK = 4
 HALVES = K // P
-W_ROWS = 4
 WARM = 64
 
 
@@ -44,33 +43,37 @@ def tile_moe_qkb_kernel(
         slot_scales = {n: keep.tile([P, S], U8, name="slot_scales_" + n, align_bytes=64) for n in names}
         w_words = {n: keep.tile([P, E, 2 * K], U8, name="w_words_" + n, align_bytes=64) for n in "qk"}
         w_scales_both = keep.tile([P, 2, E, K], U8, name="w_scales_both", align_bytes=64)
-        wv_raw = [keep.tile([P, PACK, K], F32, name="wv_raw_%d" % e) for e in range(E)]
+        wv_raw = [keep.tile([P, PACK, K], F32, name="wv_raw_%d" % e, tag="stage_%d" % e) for e in range(E)]
         wv_bf = [keep.tile([P, K, PACK], BF16, name="wv_bf_%d" % e, align_bytes=64) for e in range(E)]
         wv_codes = [keep.tile([P, K], U32, name="wv_codes_%d" % e, align_bytes=64) for e in range(E)]
         wv_scales = [keep.tile([P, K], U8, name="wv_scales_%d" % e, align_bytes=64) for e in range(E)]
         gate_sb = keep.tile([P, S], F32, name="gate_sb")
-        sums = [keep.tile([P, S], F32, name="sums_%d" % h) for h in range(HALVES)]
+        sums = {}
         result = [keep.tile([P, T], F32, name="result_%d" % h) for h in range(HALVES)]
         acc = [[psum.tile([P, C], F32, name="acc_%d_%d" % (e, h)) for h in range(HALVES)] for e in range(E)]
 
-        def load_words(n):
-            nc.sync.dma_start(tok_words[n][:], g_words[n][0].rearrange("p t d -> p (t d)").bitcast(I32))
+        w_src = {"q": (wq_words, wq_scales), "k": (wk_words, wk_scales)}
 
-        def load_scales(n, queue, which):
+        def load_words(n, queue):
+            queue.dma_start(tok_words[n][:], g_words[n][0].rearrange("p t d -> p (t d)").bitcast(I32))
+
+        def load_scales(n, r, queue):
             rows = g_scales[n][0].rearrange("(q r) t -> r q t", r=4)
-            for r in which:
-                queue.dma_start(tok_scales[n][r:P:32, :].bitcast(I32), rows[r].bitcast(I32))
+            queue.dma_start(tok_scales[n][r:P:32, :].bitcast(I32), rows[r].bitcast(I32))
 
-        def load_wv(e):
-            nc.sync.dma_start(wv_raw[e][:], wv[e].rearrange("(p j) c -> p j c", j=PACK))
+        def load_wv(e, queue):
+            queue.dma_start(wv_raw[e][:], wv[e].rearrange("(p j) c -> p j c", j=PACK))
 
-        def load_w_words(n, src):
-            nc.sync.dma_start(w_words[n][:].bitcast(I32), src.rearrange("e s p b -> p (e s) b").bitcast(I32))
+        def load_w_words(n, a, b, queue):
+            src = w_src[n][0][a:b].rearrange("e s p b -> p (e s) b")
+            queue.dma_start(w_words[n][:, a:b, :].bitcast(I32), src.bitcast(I32))
 
-        def load_w_scales(n, src):
-            rows = src.rearrange("e s (q r) c -> r q (e s) c", r=4)
-            for r in range(W_ROWS):
-                nc.gpsimd.dma_start(w_scales_both[r:P:32, "qk".index(n), :, :].bitcast(I32), rows[r].bitcast(I32))
+        def load_w_scales(n, r, queue):
+            rows = w_src[n][1].rearrange("e s (q r) c -> r q (e s) c", r=4)
+            queue.dma_start(w_scales_both[r:P:32, "qk".index(n), :, :].bitcast(I32), rows[r].bitcast(I32))
+
+        def load_gate(a, b, queue):
+            queue.dma_start(gate_sb[:, a * C : b * C], gate[:, a * C : b * C])
 
         def gather_words(n, a, b):
             window = tok_words[n][:].bitcast(U32).indirect(offsets[:, a // 16 : b // 16])
@@ -93,7 +96,7 @@ def tile_moe_qkb_kernel(
                 in_=wv_bf[e][:].rearrange("p c j -> p (c j)"),
             )
 
-        def product(n, e, h):
+        def product(n, e, h, start, stop):
             slots = slice(e * C, (e + 1) * C)
             cols = slice(h * P, (h + 1) * P)
             if n == "v":
@@ -104,79 +107,114 @@ def tile_moe_qkb_kernel(
             nc.tensor.matmul_mx(
                 out=acc[e][h][:], lhsT=lhsT, lhsT_scale=lhsT_scale,
                 rhs=slot_words[n][:, slots].bitcast(FP8X4), rhs_scale=slot_scales[n][:, slots],
-                start=(n == "q"), stop=(n == "v"),
+                start=start, stop=stop,
             )
 
         def scatter(h, a, b):
-            window = result[h][:].indirect(offsets[:, a // 16 : b // 16])
-            nc.vector.tensor_tensor(window, sums[h][:, a:b], gate_sb[:, a:b], MULT)
+            window = result[h][:].indirect(offsets[:, a * C // 16 : b * C // 16])
+            nc.vector.tensor_tensor(window, sums[h, a][:], gate_sb[:, a * C : b * C], MULT)
 
-        def evacuate(e, h):
-            nc.scalar.copy(sums[h][:, e * C : (e + 1) * C], acc[e][h][:])
-
-        def finish(e):
-            for h in range(HALVES):
-                product("v", e, h)
-            for h in range(HALVES):
-                evacuate(e, h)
-
-        nc.vector.memset(tok_scales["q"][:].bitcast(I32), 0)
+        nc.vector.memset(tok_scales["v"][:].bitcast(I32), 0)
         nc.vector.memset(result[0][:, :WARM], 0.0)
+        nc.vector.memset(tok_scales["q"][:].bitcast(I32), 0)
         nc.vector.memset(w_scales_both[:].rearrange("p n e c -> p (n e c)").bitcast(I32), 0)
         nc.vector.memset(tok_scales["k"][:].bitcast(I32), 0)
-        nc.vector.memset(tok_scales["v"][:].bitcast(I32), 0)
         nc.vector.memset(result[0][:, WARM:], 0.0)
-        nc.vector.memset(result[1][:, WARM:], 0.0)
-
-        load_scales("q", nc.scalar, range(4))
         nc.scalar.copy(result[1][:, :WARM], result[0][:, :WARM])
-        load_w_scales("q", wq_scales)
-        load_w_scales("k", wk_scales)
-
-        load_words("q")
-        load_words("k")
-        load_wv(0)
-        load_scales("k", nc.sync, (0, 1))
-        load_words("v")
-        load_scales("k", nc.sync, (2, 3))
-        load_wv(1)
-        load_scales("v", nc.sync, range(4))
-        load_w_words("q", wq_words)
-        load_w_words("k", wk_words)
-        load_wv(2)
-        nc.sync.dma_start(gate_sb[:], gate)
-        load_wv(3)
-
-        gather_words("q", 0, S)
-        gather_scales("q", 0, S)
-        gather_words("k", 0, S)
+        nc.scalar.copy(result[1][:, WARM:], result[0][:, WARM:])
+        load_words("k", nc.sync)
+        load_scales("v", 0, nc.sync)
+        load_scales("v", 1, nc.sync)
+        load_scales("v", 2, nc.sync)
+        load_scales("v", 3, nc.sync)
+        load_words("q", nc.sync)
+        load_scales("q", 0, nc.sync)
+        load_wv(1, nc.sync)
+        load_scales("q", 1, nc.sync)
+        load_scales("q", 2, nc.sync)
+        load_scales("q", 3, nc.sync)
+        load_w_scales("q", 0, nc.sync)
+        load_words("v", nc.sync)
+        load_w_scales("q", 1, nc.sync)
+        load_w_words("q", 0, 2, nc.sync)
+        load_w_scales("q", 2, nc.sync)
+        load_w_scales("q", 3, nc.sync)
+        load_wv(0, nc.sync)
+        load_scales("k", 0, nc.sync)
+        load_scales("k", 1, nc.sync)
+        load_scales("k", 2, nc.sync)
+        load_scales("k", 3, nc.sync)
+        load_w_scales("k", 0, nc.sync)
+        load_wv(2, nc.sync)
+        load_gate(2, 4, nc.sync)
+        load_w_words("k", 0, 2, nc.sync)
+        load_w_scales("k", 1, nc.sync)
+        load_w_scales("k", 2, nc.sync)
+        load_w_scales("k", 3, nc.sync)
+        load_gate(0, 2, nc.sync)
+        load_w_words("q", 2, 4, nc.sync)
+        load_wv(3, nc.sync)
+        load_w_words("k", 2, 4, nc.sync)
+        gather_words("q", 0 * C, 4 * C)
+        gather_words("k", 0 * C, 4 * C)
+        gather_words("v", 0 * C, 4 * C)
+        gather_scales("q", 0 * C, 4 * C)
+        gather_scales("k", 0 * C, 1 * C)
+        gather_scales("k", 1 * C, 4 * C)
         interleave(0)
         quantise(0)
-        gather_words("v", 0, S)
-        gather_scales("k", 0, S)
         interleave(1)
         quantise(1)
-        gather_scales("v", 0, C)
-        gather_scales("v", C, S)
-
-        for n in "qk":
-            for e in range(E):
-                for h in range(HALVES):
-                    product(n, e, h)
-        finish(0)
-        finish(1)
-        scatter(0, 0, C)
-        scatter(0, C, 2 * C)
+        gather_scales("v", 0 * C, 4 * C)
+        product("q", 0, 0, True, False)
+        product("v", 0, 0, False, False)
+        product("k", 0, 0, False, True)
+        product("q", 1, 0, True, False)
+        product("v", 1, 0, False, False)
+        product("k", 1, 0, False, True)
+        product("q", 0, 1, True, False)
+        product("v", 0, 1, False, False)
+        product("k", 0, 1, False, True)
+        product("q", 1, 1, True, False)
+        product("v", 1, 1, False, False)
+        product("k", 1, 1, False, True)
+        sums[0, 0] = keep.tile([P, 1 * C], F32, name="sums_0_0")
+        nc.scalar.copy(sums[0, 0][:, 0 * C : 1 * C], acc[0][0][:])
+        sums[0, 1] = keep.tile([P, 1 * C], F32, name="sums_0_1")
+        nc.scalar.copy(sums[0, 1][:, 0 * C : 1 * C], acc[1][0][:])
+        scatter(0, 0, 1)
+        scatter(0, 1, 2)
         interleave(2)
         quantise(2)
+        sums[1, 0] = keep.tile([P, 1 * C], F32, name="sums_1_0", tag="stage_2")
+        nc.scalar.copy(sums[1, 0][:, 0 * C : 1 * C], acc[0][1][:])
+        scatter(1, 0, 1)
         interleave(3)
         quantise(3)
-        finish(2)
-        finish(3)
-        scatter(1, 0, C)
-        scatter(1, C, 2 * C)
-        scatter(0, 2 * C, 3 * C)
-        scatter(0, 3 * C, S)
-        nc.sync.dma_start(out[0:P, :], result[0][:])
-        scatter(1, 2 * C, S)
-        nc.sync.dma_start(out[P : 2 * P, :], result[1][:])
+        sums[1, 1] = keep.tile([P, 1 * C], F32, name="sums_1_1", tag="stage_3")
+        nc.scalar.copy(sums[1, 1][:, 0 * C : 1 * C], acc[1][1][:])
+        scatter(1, 1, 2)
+        product("q", 2, 0, True, False)
+        product("k", 2, 0, False, False)
+        product("v", 2, 0, False, True)
+        product("q", 2, 1, True, False)
+        product("k", 2, 1, False, False)
+        product("v", 2, 1, False, True)
+        sums[0, 2] = keep.tile([P, 1 * C], F32, name="sums_0_2")
+        nc.scalar.copy(sums[0, 2][:, 0 * C : 1 * C], acc[2][0][:])
+        sums[1, 2] = keep.tile([P, 2 * C], F32, name="sums_1_2")
+        nc.scalar.copy(sums[1, 2][:, 0 * C : 1 * C], acc[2][1][:])
+        product("q", 3, 0, True, False)
+        product("k", 3, 0, False, False)
+        product("v", 3, 0, False, True)
+        product("q", 3, 1, True, False)
+        product("k", 3, 1, False, False)
+        product("v", 3, 1, False, True)
+        sums[0, 3] = keep.tile([P, 1 * C], F32, name="sums_0_3")
+        nc.scalar.copy(sums[0, 3][:, 0 * C : 1 * C], acc[3][0][:])
+        nc.scalar.copy(sums[1, 2][:, 1 * C : 2 * C], acc[3][1][:])
+        scatter(0, 2, 3)
+        scatter(0, 3, 4)
+        nc.sync.dma_start(out[0 * P : 1 * P, :], result[0][:])
+        scatter(1, 2, 4)
+        nc.sync.dma_start(out[1 * P : 2 * P, :], result[1][:])

@@ -114,44 +114,43 @@ def tile_moe_qkb_kernel(
             window = result[h][:].indirect(offsets[:, a * C // 16 : b * C // 16])
             nc.vector.tensor_tensor(window, sums[h, a][:], gate_sb[:, a * C : b * C], MULT)
 
-        nc.vector.memset(tok_scales["v"][:].bitcast(I32), 0)
-        nc.vector.memset(result[0][:, :WARM], 0.0)
         nc.vector.memset(tok_scales["q"][:].bitcast(I32), 0)
+        nc.vector.memset(result[0][:, :WARM], 0.0)
         nc.vector.memset(w_scales_both[:].rearrange("p n e c -> p (n e c)").bitcast(I32), 0)
+        nc.vector.memset(tok_scales["v"][:].bitcast(I32), 0)
         nc.vector.memset(tok_scales["k"][:].bitcast(I32), 0)
         nc.vector.memset(result[0][:, WARM:], 0.0)
+        load_w_scales("q", 0, nc.gpsimd)
+        load_w_scales("q", 1, nc.gpsimd)
+        load_w_scales("q", 2, nc.gpsimd)
+        load_w_scales("q", 3, nc.gpsimd)
         nc.scalar.copy(result[1][:, :WARM], result[0][:, :WARM])
         nc.scalar.copy(result[1][:, WARM:], result[0][:, WARM:])
-        load_words("k", nc.sync)
+        load_words("q", nc.sync)
+        load_scales("q", 0, nc.sync)
+        load_scales("q", 1, nc.sync)
+        load_scales("q", 2, nc.sync)
+        load_scales("q", 3, nc.sync)
+        load_wv(0, nc.sync)
+        load_words("v", nc.sync)
         load_scales("v", 0, nc.sync)
         load_scales("v", 1, nc.sync)
         load_scales("v", 2, nc.sync)
         load_scales("v", 3, nc.sync)
-        load_words("q", nc.sync)
-        load_scales("q", 0, nc.sync)
         load_wv(1, nc.sync)
-        load_scales("q", 1, nc.sync)
-        load_scales("q", 2, nc.sync)
-        load_scales("q", 3, nc.sync)
-        load_w_scales("q", 0, nc.sync)
-        load_words("v", nc.sync)
-        load_w_scales("q", 1, nc.sync)
-        load_w_words("q", 0, 2, nc.sync)
-        load_w_scales("q", 2, nc.sync)
-        load_w_scales("q", 3, nc.sync)
-        load_wv(0, nc.sync)
+        load_words("k", nc.sync)
         load_scales("k", 0, nc.sync)
         load_scales("k", 1, nc.sync)
         load_scales("k", 2, nc.sync)
         load_scales("k", 3, nc.sync)
-        load_w_scales("k", 0, nc.sync)
+        load_w_words("q", 0, 2, nc.sync)
         load_wv(2, nc.sync)
-        load_gate(2, 4, nc.sync)
-        load_w_words("k", 0, 2, nc.sync)
+        load_w_scales("k", 0, nc.sync)
         load_w_scales("k", 1, nc.sync)
         load_w_scales("k", 2, nc.sync)
         load_w_scales("k", 3, nc.sync)
-        load_gate(0, 2, nc.sync)
+        load_w_words("k", 0, 2, nc.sync)
+        load_gate(0, 4, nc.sync)
         load_w_words("q", 2, 4, nc.sync)
         load_wv(3, nc.sync)
         load_w_words("k", 2, 4, nc.sync)
@@ -182,13 +181,13 @@ def tile_moe_qkb_kernel(
         nc.scalar.copy(sums[0, 0][:, 0 * C : 1 * C], acc[0][0][:])
         sums[0, 1] = keep.tile([P, 1 * C], F32, name="sums_0_1")
         nc.scalar.copy(sums[0, 1][:, 0 * C : 1 * C], acc[1][0][:])
+        sums[1, 0] = keep.tile([P, 1 * C], F32, name="sums_1_0")
+        nc.scalar.copy(sums[1, 0][:, 0 * C : 1 * C], acc[0][1][:])
         scatter(0, 0, 1)
+        scatter(1, 0, 1)
         scatter(0, 1, 2)
         interleave(2)
         quantise(2)
-        sums[1, 0] = keep.tile([P, 1 * C], F32, name="sums_1_0", tag="stage_2")
-        nc.scalar.copy(sums[1, 0][:, 0 * C : 1 * C], acc[0][1][:])
-        scatter(1, 0, 1)
         interleave(3)
         quantise(3)
         sums[1, 1] = keep.tile([P, 1 * C], F32, name="sums_1_1", tag="stage_3")

from contextlib import ExitStack

import concourse.mybir as mybir

K, T, E, C, N = 256, 1024, 4, 128, 512
S = E * C
FLOPS = 2 * 3 * N * K * S

F32 = mybir.dt.float32
BF16 = mybir.dt.bfloat16
I32 = mybir.dt.int32
U32 = mybir.dt.uint32
U16 = mybir.dt.uint16
U8 = mybir.dt.uint8
FP8X4 = mybir.dt.float8_e4m3fn_x4
FP4X4 = mybir.dt.float4_e2m1fn_x4
MULT = mybir.AluOpType.mult

P = 128
PACK = 4
HALVES = K // P
WARM = 64


def tile_moe_qkb_kernel(
    tc, dq_words, dq_scales, dk_words, dk_scales, dv_words, dv_scales,
    wq_words, wq_scales, wk_words, wk_scales, wv, gate, offs, out,
):
    nc = tc.nc
    with ExitStack() as ctx:
        keep = ctx.enter_context(tc.tile_pool(name="keep", bufs=1))
        psum = ctx.enter_context(tc.psum_pool(name="psum", bufs=1))

        offsets = keep.tile([P, S // 16], U16, name="offsets")
        nc.sync.dma_start(offsets[:], offs)

        names = ("q", "k", "v")
        g_words = dict(zip(names, (dq_words, dk_words, dv_words)))
        g_scales = dict(zip(names, (dq_scales, dk_scales, dv_scales)))
        tok_words = {n: keep.tile([P, T], I32, name="tok_words_" + n, align_bytes=64) for n in names}
        tok_scales = {n: keep.tile([P, T], U8, name="tok_scales_" + n, align_bytes=64) for n in names}
        slot_words = {n: keep.tile([P, S], U32, name="slot_words_" + n, align_bytes=64) for n in names}
        slot_scales = {n: keep.tile([P, S], U8, name="slot_scales_" + n, align_bytes=64) for n in names}
        w_words = {n: keep.tile([P, E, 2 * K], U8, name="w_words_" + n, align_bytes=64) for n in "qk"}
        w_scales_both = keep.tile([P, 2, E, K], U8, name="w_scales_both", align_bytes=64)
        wv_raw = [keep.tile([P, PACK, K], F32, name="wv_raw_%d" % e, tag="stage_%d" % e) for e in range(E)]
        wv_bf = [keep.tile([P, K, PACK], BF16, name="wv_bf_%d" % e, align_bytes=64) for e in range(E)]
        wv_codes = [keep.tile([P, K], U32, name="wv_codes_%d" % e, align_bytes=64) for e in range(E)]
        wv_scales = [keep.tile([P, K], U8, name="wv_scales_%d" % e, align_bytes=64) for e in range(E)]
        gate_sb = keep.tile([P, S], F32, name="gate_sb")
        sums = {}
        result = [keep.tile([P, T], F32, name="result_%d" % h) for h in range(HALVES)]
        acc = [[psum.tile([P, C], F32, name="acc_%d_%d" % (e, h)) for h in range(HALVES)] for e in range(E)]

        w_src = {"q": (wq_words, wq_scales), "k": (wk_words, wk_scales)}

        def load_words(n, queue):
            queue.dma_start(tok_words[n][:], g_words[n][0].rearrange("p t d -> p (t d)").bitcast(I32))

        def load_scales(n, r, queue):
            rows = g_scales[n][0].rearrange("(q r) t -> r q t", r=4)
            queue.dma_start(tok_scales[n][r:P:32, :].bitcast(I32), rows[r].bitcast(I32))

        def load_wv(e, queue):
            queue.dma_start(wv_raw[e][:], wv[e].rearrange("(p j) c -> p j c", j=PACK))

        def load_w_words(n, a, b, queue):
            src = w_src[n][0][a:b].rearrange("e s p b -> p (e s) b")
            queue.dma_start(w_words[n][:, a:b, :].bitcast(I32), src.bitcast(I32))

        def load_w_scales(n, r, queue):
            rows = w_src[n][1].rearrange("e s (q r) c -> r q (e s) c", r=4)
            queue.dma_start(w_scales_both[r:P:32, "qk".index(n), :, :].bitcast(I32), rows[r].bitcast(I32))

        def load_gate(a, b, queue):
            queue.dma_start(gate_sb[:, a * C : b * C], gate[:, a * C : b * C])

        def gather_words(n, a, b):
            window = tok_words[n][:].bitcast(U32).indirect(offsets[:, a // 16 : b // 16])
            nc.vector.tensor_copy(slot_words[n][:, a:b], window)

        def gather_scales(n, a, b):
            window = tok_scales[n][:].indirect(offsets[:, a // 16 : b // 16])
            nc.vector.tensor_copy(slot_scales[n][:, a:b], window)

        def interleave(e):
            nc.scalar.copy(
                wv_bf[e][:].rearrange("p (c i) j -> p c j i", i=4),
                wv_raw[e][:].rearrange("p j (c i) -> p c j i", i=4),
            )

        def quantise(e):
            nc.vector.quantize_mx(
                out=wv_codes[e][:].bitcast(FP8X4),
                scales=wv_scales[e][:],
                in_=wv_bf[e][:].rearrange("p c j -> p (c j)"),
            )

        def product(n, e, h, start, stop):
            slots = slice(e * C, (e + 1) * C)
            cols = slice(h * P, (h + 1) * P)
            if n == "v":
                lhsT, lhsT_scale = wv_codes[e][:, cols].bitcast(FP8X4), wv_scales[e][:, cols]
            else:
                lhsT = w_words[n][:, e, 2 * h * P : 2 * (h + 1) * P].bitcast(FP4X4)
                lhsT_scale = w_scales_both[:, "qk".index(n), e, cols]
            nc.tensor.matmul_mx(
                out=acc[e][h][:], lhsT=lhsT, lhsT_scale=lhsT_scale,
                rhs=slot_words[n][:, slots].bitcast(FP8X4), rhs_scale=slot_scales[n][:, slots],
                start=start, stop=stop,
            )

        def scatter(h, a, b):
            window = result[h][:].indirect(offsets[:, a * C // 16 : b * C // 16])
            nc.vector.tensor_tensor(window, sums[h, a][:], gate_sb[:, a * C : b * C], MULT)

        nc.vector.memset(tok_scales["q"][:].bitcast(I32), 0)
        nc.vector.memset(result[0][:, :WARM], 0.0)
        nc.vector.memset(w_scales_both[:].rearrange("p n e c -> p (n e c)").bitcast(I32), 0)
        nc.vector.memset(tok_scales["v"][:].bitcast(I32), 0)
        nc.vector.memset(tok_scales["k"][:].bitcast(I32), 0)
        nc.vector.memset(result[0][:, WARM:], 0.0)
        load_w_scales("q", 0, nc.gpsimd)
        load_w_scales("q", 1, nc.gpsimd)
        load_w_scales("q", 2, nc.gpsimd)
        load_w_scales("q", 3, nc.gpsimd)
        nc.scalar.copy(result[1][:, :WARM], result[0][:, :WARM])
        nc.scalar.copy(result[1][:, WARM:], result[0][:, WARM:])
        load_words("q", nc.sync)
        load_scales("q", 0, nc.sync)
        load_scales("q", 1, nc.sync)
        load_scales("q", 2, nc.sync)
        load_scales("q", 3, nc.sync)
        load_wv(0, nc.sync)
        load_words("v", nc.sync)
        load_scales("v", 0, nc.sync)
        load_scales("v", 1, nc.sync)
        load_scales("v", 2, nc.sync)
        load_scales("v", 3, nc.sync)
        load_wv(1, nc.sync)
        load_words("k", nc.sync)
        load_scales("k", 0, nc.sync)
        load_scales("k", 1, nc.sync)
        load_scales("k", 2, nc.sync)
        load_scales("k", 3, nc.sync)
        load_w_words("q", 0, 2, nc.sync)
        load_wv(2, nc.sync)
        load_w_scales("k", 0, nc.sync)
        load_w_scales("k", 1, nc.sync)
        load_w_scales("k", 2, nc.sync)
        load_w_scales("k", 3, nc.sync)
        load_w_words("k", 0, 2, nc.sync)
        load_gate(0, 4, nc.sync)
        load_w_words("q", 2, 4, nc.sync)
        load_wv(3, nc.sync)
        load_w_words("k", 2, 4, nc.sync)
        gather_words("q", 0 * C, 4 * C)
        gather_words("k", 0 * C, 4 * C)
        gather_words("v", 0 * C, 4 * C)
        gather_scales("q", 0 * C, 4 * C)
        gather_scales("k", 0 * C, 1 * C)
        gather_scales("k", 1 * C, 4 * C)
        interleave(0)
        quantise(0)
        interleave(1)
        quantise(1)
        gather_scales("v", 0 * C, 4 * C)
        product("q", 0, 0, True, False)
        product("v", 0, 0, False, False)
        product("k", 0, 0, False, True)
        product("q", 1, 0, True, False)
        product("v", 1, 0, False, False)
        product("k", 1, 0, False, True)
        product("q", 0, 1, True, False)
        product("v", 0, 1, False, False)
        product("k", 0, 1, False, True)
        product("q", 1, 1, True, False)
        product("v", 1, 1, False, False)
        product("k", 1, 1, False, True)
        sums[0, 0] = keep.tile([P, 1 * C], F32, name="sums_0_0")
        nc.scalar.copy(sums[0, 0][:, 0 * C : 1 * C], acc[0][0][:])
        sums[0, 1] = keep.tile([P, 1 * C], F32, name="sums_0_1")
        nc.scalar.copy(sums[0, 1][:, 0 * C : 1 * C], acc[1][0][:])
        sums[1, 0] = keep.tile([P, 1 * C], F32, name="sums_1_0")
        nc.scalar.copy(sums[1, 0][:, 0 * C : 1 * C], acc[0][1][:])
        scatter(0, 0, 1)
        scatter(1, 0, 1)
        scatter(0, 1, 2)
        interleave(2)
        quantise(2)
        interleave(3)
        quantise(3)
        sums[1, 1] = keep.tile([P, 1 * C], F32, name="sums_1_1", tag="stage_3")
        nc.scalar.copy(sums[1, 1][:, 0 * C : 1 * C], acc[1][1][:])
        scatter(1, 1, 2)
        product("q", 2, 0, True, False)
        product("k", 2, 0, False, False)
        product("v", 2, 0, False, True)
        product("q", 2, 1, True, False)
        product("k", 2, 1, False, False)
        product("v", 2, 1, False, True)
        sums[0, 2] = keep.tile([P, 1 * C], F32, name="sums_0_2")
        nc.scalar.copy(sums[0, 2][:, 0 * C : 1 * C], acc[2][0][:])
        sums[1, 2] = keep.tile([P, 2 * C], F32, name="sums_1_2")
        nc.scalar.copy(sums[1, 2][:, 0 * C : 1 * C], acc[2][1][:])
        product("q", 3, 0, True, False)
        product("k", 3, 0, False, False)
        product("v", 3, 0, False, True)
        product("q", 3, 1, True, False)
        product("k", 3, 1, False, False)
        product("v", 3, 1, False, True)
        sums[0, 3] = keep.tile([P, 1 * C], F32, name="sums_0_3")
        nc.scalar.copy(sums[0, 3][:, 0 * C : 1 * C], acc[3][0][:])
        nc.scalar.copy(sums[1, 2][:, 1 * C : 2 * C], acc[3][1][:])
        scatter(0, 2, 3)
        scatter(0, 3, 4)
        nc.sync.dma_start(out[0 * P : 1 * P, :], result[0][:])
        scatter(1, 2, 4)
        nc.sync.dma_start(out[1 * P : 2 * P, :], result[1][:])
